import numpy as np
import ml_dtypes


def mxq(x, axis, fmt="e4m3"):
    dtype, down = {"e4m3": (ml_dtypes.float8_e4m3fn, 7), "e5m2": (ml_dtypes.float8_e5m2, 14)}[fmt]
    v = np.moveaxis(np.asarray(x, np.float32).astype(ml_dtypes.bfloat16).astype(np.float64), axis, -1)
    blocks = v.reshape(v.shape[:-1] + (-1, 32))
    amax = np.abs(blocks).max(-1, keepdims=True)
    byte = np.maximum(np.where(amax > 0, np.frexp(amax)[1] - 1 + 127, 0) - down, 1)
    scale = np.exp2(byte - 127.0)
    codes = (blocks / scale).astype(np.float32).astype(dtype).astype(np.float64)
    return np.moveaxis((codes * scale).reshape(v.shape), -1, axis)


WIDE = False


def mx_kscale(k, group=512):
    if not WIDE:
        return np.ones(k)
    levels = np.array([10, -10, 5, -5, 0])
    if group != 512:
        return np.exp2(np.random.permutation(np.resize(levels, k // group))).repeat(group)
    if k % 512:
        return np.exp2(np.random.permutation(np.resize(levels, k // 32))).repeat(32)
    a = np.empty((k // 512, 16))
    for p in range(k // 512):
        a[p, :8] = np.random.permutation(np.resize(levels, 8))
        for g in range(8):
            far = levels[np.abs(levels - a[p, g]) >= 10]
            a[p, g + 8] = far[np.random.randint(len(far))]
    return np.exp2(a.ravel()).repeat(32)


def f64(x):
    return np.asarray(x).astype(np.float64)


G, D, M, O, N = 2, 256, 128, 256, 512


def setup_inputs():
    n = np.random.standard_normal
    s_d = mx_kscale(D, 0)
    s_o = mx_kscale(O, 0)
    return {
        "x": (n((G, D, N)) * s_d[:, None]).astype(np.float32),
        "w1": (n((G, D, M)) / np.sqrt(D) / s_d[:, None]).astype(np.float32),
        "w2": (n((G, D, M)) / np.sqrt(D) / s_d[:, None]).astype(np.float32),
        "w3": (n((G, D, M)) / np.sqrt(D) / s_d[:, None]).astype(np.float32),
        "wo": (n((G, O, M)) / np.sqrt(O) / s_o[:, None]).astype(np.float32),
        "dy": (n((G, O, N)) * s_o[:, None]).astype(np.float32),
        "og": (np.random.uniform(0.3, 1.0, (G, M, 1))).astype(np.float32),
        "base": (0.2 * n((G, M, N))).astype(np.float32),
    }


def reference(x, w1, w2, w3, wo, dy, og, base):
    w1q = mxq(f64(w1), 1, "e4m3")
    xq = mxq(f64(x), 1, "e4m3")
    z1 = w1q.transpose(0, 2, 1) @ xq
    w2q = mxq(f64(w2), 1, "e4m3")
    z2 = w2q.transpose(0, 2, 1) @ xq
    w3q = mxq(f64(w3), 1, "e4m3")
    z3 = w3q.transpose(0, 2, 1) @ xq
    se = np.exp(z1) + np.exp(z2) + np.exp(z3)
    woq = mxq(f64(wo), 1, "e4m3")
    dyq = mxq(f64(dy), 1, "e4m3")
    c0 = woq.transpose(0, 2, 1) @ dyq
    dse = c0 * np.tanh(z1) / se
    dz1 = c0 * np.log(se) * (1.0 - np.square(np.tanh(z1))) + dse * np.exp(z1)
    kdz1 = dz1 * 2.0
    kdse = kdz1 * np.exp(z1)
    kse = kdz1 * (1.0 - np.square(np.tanh(z1))) * c0 / se - kdse * c0 * np.tanh(z1) / np.square(se)
    kz1 = kdz1 * c0 * np.log(se) * (-1.0) * np.tanh(z1) * 2.0 * (1.0 - np.square(np.tanh(z1))) + kdz1 * dse * np.exp(z1) + kdse / se * c0 * (1.0 - np.square(np.tanh(z1))) + kse * np.exp(z1)
    y = kz1 * f64(og) + f64(base)
    return y

@@ -1,0 +1,159 @@
+from contextlib import ExitStack
+
+import concourse.mybir as mybir
+
+G, D, M, N = 2, 256, 128, 512
+FLOPS = 4 * 2 * G * D * M * N
+
+F32 = mybir.dt.float32
+BF16 = mybir.dt.bfloat16
+U32 = mybir.dt.uint32
+U8 = mybir.dt.uint8
+FP8X4 = mybir.dt.float8_e4m3fn_x4
+ACT = mybir.ActivationFunctionType
+ALU = mybir.AluOpType
+
+P = 128
+PACK = 4
+ROWS = D // PACK
+X_SPLIT = 352
+PIECE = 256
+
+
+def tile_rows_gpsoftmaxthree_kernel(tc, x, w1, w2, w3, wo, dy, og, base, out):
+    nc = tc.nc
+    with ExitStack() as ctx:
+        sb = ctx.enter_context(tc.tile_pool(name="sb", bufs=1))
+        ps = ctx.enter_context(tc.psum_pool(name="ps", bufs=1))
+        ctx.enter_context(tc.manual_schedule())
+
+        def load(name, src):
+            width = src.shape[2]
+            raw = sb.tile([P, PACK, width], F32, name=name + "_raw", align_bytes=64)
+            nc.sync.dma_start(out=raw[:], in_=src.rearrange("g (p j) w -> (g p) j w", j=PACK))
+            grouped = sb.tile([P, width, PACK], BF16, name=name + "_bf", align_bytes=64)
+            codes = sb.tile([P, width], U32, name=name + "_codes", align_bytes=64)
+            scales = sb.tile([P, width], U8, name=name + "_scales", align_bytes=64)
+            return {"raw": raw, "grouped": grouped, "codes": codes, "scales": scales, "width": width}
+
+        def interleave(copy, operand, c0, c1):
+            copy(
+                out=operand["grouped"][:, c0:c1, :].rearrange("p (c i) j -> p c j i", i=4),
+                in_=operand["raw"][:, :, c0:c1].rearrange("p j (c i) -> p c j i", i=4),
+            )
+
+        def quantize(operand):
+            nc.vector.quantize_mx(
+                out=operand["codes"][:].bitcast(FP8X4),
+                scales=operand["scales"][:],
+                in_=operand["grouped"][:].rearrange("p w j -> p (w j)"),
+            )
+
+        def product(name, weights, moving):
+            sums = []
+            for g in range(G):
+                rows = slice(g * ROWS, (g + 1) * ROWS)
+                acc = ps.tile([M, N], F32, name=name + str(g))
+                nc.tensor.matmul_mx(
+                    out=acc[:],
+                    lhsT=weights["codes"][rows, :].bitcast(FP8X4),
+                    lhsT_scale=weights["scales"][rows, :],
+                    rhs=moving["codes"][rows, :].bitcast(FP8X4),
+                    rhs_scale=moving["scales"][rows, :],
+                    start=True,
+                    stop=True,
+                )
+                sums.append(acc)
+            return sums
+
+        def per_group(name):
+            tiles = []
+            for g in range(G):
+                t = sb.tile([M, N], F32, name=name + str(g))
+                tiles.append(t)
+            return tiles
+
+        def fused(dst, a, scalar, op0, b, op1):
+            nc.vector.scalar_tensor_tensor(out=dst, in0=a, scalar=scalar, in1=b, op0=op0, op1=op1)
+
+        w1o = load("w1", w1)
+        xo = load("x", x)
+        w2o = load("w2", w2)
+        w3o = load("w3", w3)
+        woo = load("wo", wo)
+        dyo = load("dy", dy)
+        gain = sb.tile([M, G, 1], F32, name="gain")
+        with nc.allow_non_contiguous_dma(reason="one gain per partition and group"):
+            nc.sync.dma_start(out=gain[:], in_=og.rearrange("g m o -> m g o"))
+        base_sb = sb.tile([M, G, N], F32, name="base_sb")
+        nc.sync.dma_start(out=base_sb[:], in_=base.rearrange("g m n -> m g n"))
+
+        interleave(nc.scalar.copy, w1o, 0, M)
+        quantize(w1o)
+        interleave(nc.vector.tensor_copy, xo, 0, X_SPLIT)
+        interleave(nc.scalar.copy, xo, X_SPLIT, N)
+        quantize(xo)
+        z1 = product("z1_", w1o, xo)
+        interleave(nc.scalar.copy, w2o, 0, M)
+        interleave(nc.vector.tensor_copy, w3o, 0, M)
+        quantize(w2o)
+        z2 = product("z2_", w2o, xo)
+        quantize(w3o)
+        z3 = product("z3_", w3o, xo)
+
+        e1, e2, e3 = per_group("e1_"), per_group("e2_"), per_group("e3_")
+        th, th2 = per_group("th_"), per_group("th2_")
+        e12, se, lse = per_group("e12_"), per_group("se_"), per_group("lse_")
+        logp, nsl = per_group("logp_"), per_group("nsl_")
+        for g in range(G):
+            nc.scalar.activation(out=e1[g][:], in_=z1[g][:], func=ACT.Exp)
+        for g in range(G):
+            nc.scalar.activation(out=th[g][:], in_=z1[g][:], func=ACT.Tanh)
+        for g in range(G):
+            nc.scalar.activation(out=e2[g][:], in_=z2[g][:], func=ACT.Exp)
+            nc.scalar.activation(out=e3[g][:], in_=z3[g][:], func=ACT.Exp)
+
+        interleave(nc.vector.tensor_copy, woo, 0, M)
+        for g in range(G):
+            nc.vector.tensor_tensor(out=th2[g][:], in0=th[g][:], in1=th[g][:], op=ALU.mult)
+        quantize(woo)
+        for g in range(G):
+            nc.vector.tensor_tensor(out=e12[g][:], in0=e1[g][:], in1=e2[g][:], op=ALU.add)
+            interleave(nc.vector.tensor_copy, dyo, g * N // G, (g + 1) * N // G)
+            nc.vector.tensor_tensor(out=se[g][:], in0=e12[g][:], in1=e3[g][:], op=ALU.add)
+        quantize(dyo)
+        c0 = product("c0_", woo, dyo)
+
+        for g in range(G):
+            nc.scalar.activation(out=lse[g][:], in_=se[g][:], func=ACT.Ln)
+        for g in range(G):
+            nc.vector.tensor_tensor(out=logp[g][:], in0=z1[g][:], in1=lse[g][:], op=ALU.subtract)
+            fused(nsl[g][:], th2[g][:], 1.0, ALU.subtract, lse[g][:], ALU.mult)
+
+        prob, sq, csq = per_group("prob_"), per_group("sq_"), per_group("csq_")
+        tp, a, t1, t2, b = per_group("tp_"), per_group("a_"), per_group("t1_"), per_group("t2_"), per_group("b_")
+        ac, abc, res = per_group("ac_"), per_group("abc_"), per_group("res_")
+        pieces = [slice(c, c + PIECE) for c in range(0, N, PIECE)]
+        for g in range(G):
+            for s in pieces:
+                nc.scalar.activation(out=prob[g][:, s], in_=logp[g][:, s], func=ACT.Exp)
+            for s in pieces:
+                nc.scalar.activation(out=sq[g][:, s], in_=prob[g][:, s], func=ACT.Square, bias=-0.5)
+            nc.scalar.activation(out=csq[g][:], in_=c0[g][:], func=ACT.Square)
+            for s in pieces:
+                nc.vector.tensor_tensor(out=tp[g][:, s], in0=th[g][:, s], in1=prob[g][:, s], op=ALU.mult)
+            for s in pieces:
+                nc.vector.tensor_tensor(out=a[g][:, s], in0=tp[g][:, s], in1=nsl[g][:, s], op=ALU.subtract)
+            for s in pieces:
+                fused(t1[g][:, s], a[g][:, s], 2.0, ALU.mult, sq[g][:, s], ALU.add)
+            for s in pieces:
+                fused(t2[g][:, s], t1[g][:, s], 0.25, ALU.subtract, th[g][:, s], ALU.mult)
+            for s in pieces:
+                fused(ac[g][:, s], a[g][:, s], gain[:, g, :], ALU.mult, csq[g][:, s], ALU.mult)
+            for s in pieces:
+                fused(b[g][:, s], prob[g][:, s], 2.0, ALU.mult, t2[g][:, s], ALU.subtract)
+            for s in pieces:
+                fused(abc[g][:, s], ac[g][:, s], 2.0, ALU.mult, b[g][:, s], ALU.mult)
+            for s in pieces:
+                nc.vector.tensor_tensor(out=res[g][:, s], in0=abc[g][:, s], in1=base_sb[:, g, s], op=ALU.add)
+                nc.sync.dma_start(out=out[g, :, s], in_=res[g][:, s])

@@ -16,8 +16,10 @@ ALU = mybir.AluOpType
 P = 128
 PACK = 4
 ROWS = D // PACK
-X_SPLIT = 352
-PIECE = 256
+HALVES = 2
+HALF = N // HALVES
+PASS_N = 128
+X_SPLIT = 176
 
 
 def tile_rows_gpsoftmaxthree_kernel(tc, x, w1, w2, w3, wo, dy, og, base, out):
@@ -34,7 +36,7 @@ def tile_rows_gpsoftmaxthree_kernel(tc, x, w1, w2, w3, wo, dy, og, base, out):
             grouped = sb.tile([P, width, PACK], BF16, name=name + "_bf", align_bytes=64)
             codes = sb.tile([P, width], U32, name=name + "_codes", align_bytes=64)
             scales = sb.tile([P, width], U8, name=name + "_scales", align_bytes=64)
-            return {"raw": raw, "grouped": grouped, "codes": codes, "scales": scales, "width": width}
+            return {"raw": raw, "grouped": grouped, "codes": codes, "scales": scales}
 
         def interleave(copy, operand, c0, c1):
             copy(
@@ -49,37 +51,49 @@ def tile_rows_gpsoftmaxthree_kernel(tc, x, w1, w2, w3, wo, dy, og, base, out):
                 in_=operand["grouped"][:].rearrange("p w j -> p (w j)"),
             )
 
-        def product(name, weights, moving):
-            sums = []
-            for g in range(G):
-                rows = slice(g * ROWS, (g + 1) * ROWS)
-                acc = ps.tile([M, N], F32, name=name + str(g))
-                nc.tensor.matmul_mx(
-                    out=acc[:],
-                    lhsT=weights["codes"][rows, :].bitcast(FP8X4),
-                    lhsT_scale=weights["scales"][rows, :],
-                    rhs=moving["codes"][rows, :].bitcast(FP8X4),
-                    rhs_scale=moving["scales"][rows, :],
-                    start=True,
-                    stop=True,
-                )
-                sums.append(acc)
-            return sums
-
-        def per_group(name):
+        def banks(name):
             tiles = []
             for g in range(G):
-                t = sb.tile([M, N], F32, name=name + str(g))
+                t = ps.tile([M, N], F32, name=name + str(g))
+                tiles.append(t)
+            return tiles
+
+        def product(sums, first, weights, moving, groups):
+            width = moving["codes"].shape[1]
+            for g in groups:
+                rows = slice(g * ROWS, (g + 1) * ROWS)
+                for c in range(0, width, PASS_N):
+                    nc.tensor.matmul_mx(
+                        out=sums[g][:, first + c : first + c + PASS_N],
+                        lhsT=weights["codes"][rows, :].bitcast(FP8X4),
+                        lhsT_scale=weights["scales"][rows, :],
+                        rhs=moving["codes"][rows, c : c + PASS_N].bitcast(FP8X4),
+                        rhs_scale=moving["scales"][rows, c : c + PASS_N],
+                        start=True,
+                        stop=True,
+                    )
+
+        def values(name):
+            tiles = []
+            for h in range(HALVES):
+                t = sb.tile([M, G, HALF], F32, name=name + str(h))
                 tiles.append(t)
             return tiles
 
         def fused(dst, a, scalar, op0, b, op1):
             nc.vector.scalar_tensor_tensor(out=dst, in0=a, scalar=scalar, in1=b, op0=op0, op1=op1)
 
+        def binary(dst, a, op, b):
+            nc.vector.tensor_tensor(out=dst, in0=a, in1=b, op=op)
+
+        half = [slice(h * HALF, (h + 1) * HALF) for h in range(HALVES)]
+        groups = range(G)
+        both = slice(0, G)
+        xa = load("xa", x[:, :, half[0]])
         w1o = load("w1", w1)
-        xo = load("x", x)
         w2o = load("w2", w2)
         w3o = load("w3", w3)
+        xb = load("xb", x[:, :, half[1]])
         woo = load("wo", wo)
         dyo = load("dy", dy)
         gain = sb.tile([M, G, 1], F32, name="gain")
@@ -88,72 +102,134 @@ def tile_rows_gpsoftmaxthree_kernel(tc, x, w1, w2, w3, wo, dy, og, base, out):
         base_sb = sb.tile([M, G, N], F32, name="base_sb")
         nc.sync.dma_start(out=base_sb[:], in_=base.rearrange("g m n -> m g n"))
 
-        interleave(nc.scalar.copy, w1o, 0, M)
+        z1, c0 = banks("z1_"), banks("c0_")
+        z23 = [banks("z23a_"), banks("z23b_")]
+        e23 = []
+        for h in range(HALVES):
+            pair = sb.tile([M, 2, G, HALF], F32, name="e23_" + str(h))
+            e23.append(pair)
+        csq = sb.tile([M, G, N], F32, name="csq")
+        e1, th, th2 = values("e1"), values("th"), values("th2")
+        e12, se, lse, logp, nsl = values("e12"), values("se"), values("lse"), values("logp"), values("nsl")
+        prob, sq, tp, a = values("prob"), values("sq"), values("tp"), values("a")
+        t1, t2, b, ac, abc, res = values("t1"), values("t2"), values("b"), values("ac"), values("abc"), values("res")
+
+        def exp_z23(h):
+            for g in groups:
+                nc.scalar.activation(
+                    out=e23[h][:, :, g, :], in_=z23[h][g][:].rearrange("m (k n) -> m k n", k=2), func=ACT.Exp
+                )
+
+        def step_e12(h):
+            binary(e12[h][:], e1[h][:], ALU.add, e23[h][:, 0])
+
+        def step_se(h):
+            binary(se[h][:], e12[h][:], ALU.add, e23[h][:, 1])
+
+        def step_logp(h):
+            for g in groups:
+                binary(logp[h][:, g], z1[g][:, half[h]], ALU.subtract, lse[h][:, g])
+
+        def step_nsl(h, g):
+            fused(nsl[h][:, g], th2[h][:, g], 1.0, ALU.subtract, lse[h][:, g], ALU.mult)
+
+        def step_tp(h, g):
+            binary(tp[h][:, g], th[h][:, g], ALU.mult, prob[h][:, g])
+
+        def step_a(h, g):
+            binary(a[h][:, g], tp[h][:, g], ALU.subtract, nsl[h][:, g])
+
+        def step_t1(h, g):
+            fused(t1[h][:, g], a[h][:, g], 2.0, ALU.mult, sq[h][:, g], ALU.add)
+
+        def step_t2(h, g):
+            fused(t2[h][:, g], t1[h][:, g], 0.25, ALU.subtract, th[h][:, g], ALU.mult)
+
+        def step_b(h, g):
+            fused(b[h][:, g], prob[h][:, g], 2.0, ALU.mult, t2[h][:, g], ALU.subtract)
+
+        def step_ac(h):
+            for g in groups:
+                fused(ac[h][:, g], a[h][:, g], gain[:, g, :], ALU.mult, csq[:, g, half[h]], ALU.mult)
+
+        def step_abc(h, g):
+            fused(abc[h][:, g], ac[h][:, g], 2.0, ALU.mult, b[h][:, g], ALU.mult)
+
+        def step_out(h):
+            for g, queue in zip(groups, (nc.sync, nc.scalar)):
+                binary(res[h][:, g], abc[h][:, g], ALU.add, base_sb[:, g, half[h]])
+                queue.dma_start(out=out[g, :, half[h]], in_=res[h][:, g])
+
+        interleave(nc.vector.tensor_copy, xa, 0, X_SPLIT)
+        interleave(nc.scalar.copy, xa, X_SPLIT, HALF)
+        interleave(nc.vector.tensor_copy, w1o, 0, M)
+        quantize(xa)
         quantize(w1o)
-        interleave(nc.vector.tensor_copy, xo, 0, X_SPLIT)
-        interleave(nc.scalar.copy, xo, X_SPLIT, N)
-        quantize(xo)
-        z1 = product("z1_", w1o, xo)
-        interleave(nc.scalar.copy, w2o, 0, M)
+        product(z1, 0, w1o, xa, groups)
+        for g in groups:
+            nc.scalar.activation(out=e1[0][:, g], in_=z1[g][:, half[0]], func=ACT.Exp)
+            nc.scalar.activation(out=th[0][:, g], in_=z1[g][:, half[0]], func=ACT.Tanh)
+        interleave(nc.vector.tensor_copy, w2o, 0, M)
         interleave(nc.vector.tensor_copy, w3o, 0, M)
         quantize(w2o)
-        z2 = product("z2_", w2o, xo)
         quantize(w3o)
-        z3 = product("z3_", w3o, xo)
+        for g in groups:
+            product(z23[0], 0, w2o, xa, [g])
+            product(z23[0], HALF, w3o, xa, [g])
+        exp_z23(0)
+        interleave(nc.vector.tensor_copy, xb, 0, HALF)
+        quantize(xb)
+        product(z1, HALF, w1o, xb, groups)
+        for g in groups:
+            product(z23[1], 0, w2o, xb, [g])
+            product(z23[1], HALF, w3o, xb, [g])
+        for g in groups:
+            nc.scalar.activation(out=e1[1][:, g], in_=z1[g][:, half[1]], func=ACT.Exp)
+        exp_z23(1)
 
-        e1, e2, e3 = per_group("e1_"), per_group("e2_"), per_group("e3_")
-        th, th2 = per_group("th_"), per_group("th2_")
-        e12, se, lse = per_group("e12_"), per_group("se_"), per_group("lse_")
-        logp, nsl = per_group("logp_"), per_group("nsl_")
-        for g in range(G):
-            nc.scalar.activation(out=e1[g][:], in_=z1[g][:], func=ACT.Exp)
-        for g in range(G):
-            nc.scalar.activation(out=th[g][:], in_=z1[g][:], func=ACT.Tanh)
-        for g in range(G):
-            nc.scalar.activation(out=e2[g][:], in_=z2[g][:], func=ACT.Exp)
-            nc.scalar.activation(out=e3[g][:], in_=z3[g][:], func=ACT.Exp)
-
+        binary(th2[0][:], th[0][:], ALU.mult, th[0][:])
+        step_e12(0)
         interleave(nc.vector.tensor_copy, woo, 0, M)
-        for g in range(G):
-            nc.vector.tensor_tensor(out=th2[g][:], in0=th[g][:], in1=th[g][:], op=ALU.mult)
+        step_se(0)
         quantize(woo)
-        for g in range(G):
-            nc.vector.tensor_tensor(out=e12[g][:], in0=e1[g][:], in1=e2[g][:], op=ALU.add)
-            interleave(nc.vector.tensor_copy, dyo, g * N // G, (g + 1) * N // G)
-            nc.vector.tensor_tensor(out=se[g][:], in0=e12[g][:], in1=e3[g][:], op=ALU.add)
+        interleave(nc.vector.tensor_copy, dyo, 0, HALF)
+        step_e12(1)
+        interleave(nc.vector.tensor_copy, dyo, HALF, N)
+        step_se(1)
+        for h in range(HALVES):
+            nc.scalar.activation(out=lse[h][:], in_=se[h][:], func=ACT.Ln)
+        step_logp(0)
         quantize(dyo)
-        c0 = product("c0_", woo, dyo)
+        product(c0, 0, woo, dyo, groups)
+        step_nsl(0, both)
+        step_logp(1)
 
-        for g in range(G):
-            nc.scalar.activation(out=lse[g][:], in_=se[g][:], func=ACT.Ln)
-        for g in range(G):
-            nc.vector.tensor_tensor(out=logp[g][:], in0=z1[g][:], in1=lse[g][:], op=ALU.subtract)
-            fused(nsl[g][:], th2[g][:], 1.0, ALU.subtract, lse[g][:], ALU.mult)
+        for g in groups:
+            nc.scalar.activation(out=prob[0][:, g], in_=logp[0][:, g], func=ACT.Exp)
+        nc.scalar.activation(out=sq[0][:], in_=prob[0][:], func=ACT.Square, bias=-0.5)
+        for g in groups:
+            nc.scalar.activation(out=th[1][:, g], in_=z1[g][:, half[1]], func=ACT.Tanh)
+        nc.scalar.activation(out=prob[1][:], in_=logp[1][:], func=ACT.Exp)
+        nc.scalar.activation(out=th2[1][:], in_=th[1][:], func=ACT.Square)
+        nc.scalar.activation(out=sq[1][:], in_=prob[1][:], func=ACT.Square, bias=-0.5)
+        for g in groups:
+            nc.scalar.activation(out=csq[:, g, :], in_=c0[g][:], func=ACT.Square)
 
-        prob, sq, csq = per_group("prob_"), per_group("sq_"), per_group("csq_")
-        tp, a, t1, t2, b = per_group("tp_"), per_group("a_"), per_group("t1_"), per_group("t2_"), per_group("b_")
-        ac, abc, res = per_group("ac_"), per_group("abc_"), per_group("res_")
-        pieces = [slice(c, c + PIECE) for c in range(0, N, PIECE)]
-        for g in range(G):
-            for s in pieces:
-                nc.scalar.activation(out=prob[g][:, s], in_=logp[g][:, s], func=ACT.Exp)
-            for s in pieces:
-                nc.scalar.activation(out=sq[g][:, s], in_=prob[g][:, s], func=ACT.Square, bias=-0.5)
-            nc.scalar.activation(out=csq[g][:], in_=c0[g][:], func=ACT.Square)
-            for s in pieces:
-                nc.vector.tensor_tensor(out=tp[g][:, s], in0=th[g][:, s], in1=prob[g][:, s], op=ALU.mult)
-            for s in pieces:
-                nc.vector.tensor_tensor(out=a[g][:, s], in0=tp[g][:, s], in1=nsl[g][:, s], op=ALU.subtract)
-            for s in pieces:
-                fused(t1[g][:, s], a[g][:, s], 2.0, ALU.mult, sq[g][:, s], ALU.add)
-            for s in pieces:
-                fused(t2[g][:, s], t1[g][:, s], 0.25, ALU.subtract, th[g][:, s], ALU.mult)
-            for s in pieces:
-                fused(ac[g][:, s], a[g][:, s], gain[:, g, :], ALU.mult, csq[g][:, s], ALU.mult)
-            for s in pieces:
-                fused(b[g][:, s], prob[g][:, s], 2.0, ALU.mult, t2[g][:, s], ALU.subtract)
-            for s in pieces:
-                fused(abc[g][:, s], ac[g][:, s], 2.0, ALU.mult, b[g][:, s], ALU.mult)
-            for s in pieces:
-                nc.vector.tensor_tensor(out=res[g][:, s], in0=abc[g][:, s], in1=base_sb[:, g, s], op=ALU.add)
-                nc.sync.dma_start(out=out[g, :, s], in_=res[g][:, s])
+        for step in (step_tp, step_a, step_t1):
+            for g in groups:
+                step(0, g)
+        step_tp(1, both)
+        step_t2(0, both)
+        step_nsl(1, both)
+        step_b(0, both)
+        step_a(1, both)
+        step_ac(0)
+        step_t1(1, both)
+        step_abc(0, both)
+        step_t2(1, both)
+        step_out(0)
+        step_b(1, both)
+        step_ac(1)
+        for g in groups:
+            step_abc(1, g)
+        step_out(1)

@@ -44,11 +44,11 @@ def tile_rows_gpsoftmaxthree_kernel(tc, x, w1, w2, w3, wo, dy, og, base, out):
                 in_=operand["raw"][:, :, c0:c1].rearrange("p j (c i) -> p c j i", i=4),
             )
 
-        def quantize(operand):
+        def quantize(operand, c0, c1):
             nc.vector.quantize_mx(
-                out=operand["codes"][:].bitcast(FP8X4),
-                scales=operand["scales"][:],
-                in_=operand["grouped"][:].rearrange("p w j -> p (w j)"),
+                out=operand["codes"][:, c0:c1].bitcast(FP8X4),
+                scales=operand["scales"][:, c0:c1],
+                in_=operand["grouped"][:, c0:c1, :].rearrange("p w j -> p (w j)"),
             )
 
         def banks(name):
@@ -96,11 +96,11 @@ def tile_rows_gpsoftmaxthree_kernel(tc, x, w1, w2, w3, wo, dy, og, base, out):
         xb = load("xb", x[:, :, half[1]])
         woo = load("wo", wo)
         dyo = load("dy", dy)
+        base_sb = sb.tile([M, G, N], F32, name="base_sb")
+        nc.sync.dma_start(out=base_sb[:], in_=base.rearrange("g m n -> m g n"))
         gain = sb.tile([M, G, 1], F32, name="gain")
         with nc.allow_non_contiguous_dma(reason="one gain per partition and group"):
             nc.sync.dma_start(out=gain[:], in_=og.rearrange("g m o -> m g o"))
-        base_sb = sb.tile([M, G, N], F32, name="base_sb")
-        nc.sync.dma_start(out=base_sb[:], in_=base.rearrange("g m n -> m g n"))
 
         z1, c0 = banks("z1_"), banks("c0_")
         z23 = [banks("z23a_"), banks("z23b_")]
@@ -163,22 +163,24 @@ def tile_rows_gpsoftmaxthree_kernel(tc, x, w1, w2, w3, wo, dy, og, base, out):
         interleave(nc.vector.tensor_copy, xa, 0, X_SPLIT)
         interleave(nc.scalar.copy, xa, X_SPLIT, HALF)
         interleave(nc.vector.tensor_copy, w1o, 0, M)
-        quantize(xa)
-        quantize(w1o)
+        quantize(xa, 0, HALF)
+        quantize(w1o, 0, M)
         product(z1, 0, w1o, xa, groups)
         for g in groups:
             nc.scalar.activation(out=e1[0][:, g], in_=z1[g][:, half[0]], func=ACT.Exp)
             nc.scalar.activation(out=th[0][:, g], in_=z1[g][:, half[0]], func=ACT.Tanh)
         interleave(nc.vector.tensor_copy, w2o, 0, M)
         interleave(nc.vector.tensor_copy, w3o, 0, M)
-        quantize(w2o)
-        quantize(w3o)
+        quantize(w2o, 0, M)
+        quantize(w3o, 0, M)
         for g in groups:
             product(z23[0], 0, w2o, xa, [g])
             product(z23[0], HALF, w3o, xa, [g])
         exp_z23(0)
-        interleave(nc.vector.tensor_copy, xb, 0, HALF)
-        quantize(xb)
+        for c in range(0, HALF, PASS_N):
+            interleave(nc.vector.tensor_copy, xb, c, c + PASS_N)
+        for c in range(0, HALF, PASS_N):
+            quantize(xb, c, c + PASS_N)
         product(z1, HALF, w1o, xb, groups)
         for g in groups:
             product(z23[1], 0, w2o, xb, [g])
@@ -191,15 +193,14 @@ def tile_rows_gpsoftmaxthree_kernel(tc, x, w1, w2, w3, wo, dy, og, base, out):
         step_e12(0)
         interleave(nc.vector.tensor_copy, woo, 0, M)
         step_se(0)
-        quantize(woo)
-        interleave(nc.vector.tensor_copy, dyo, 0, HALF)
         step_e12(1)
-        interleave(nc.vector.tensor_copy, dyo, HALF, N)
+        quantize(woo, 0, M)
         step_se(1)
+        interleave(nc.vector.tensor_copy, dyo, 0, N)
         for h in range(HALVES):
             nc.scalar.activation(out=lse[h][:], in_=se[h][:], func=ACT.Ln)
         step_logp(0)
-        quantize(dyo)
+        quantize(dyo, 0, N)
         product(c0, 0, woo, dyo, groups)
         step_nsl(0, both)
         step_logp(1)

@@ -40,8 +40,8 @@ def tile_rows_gpsoftmaxthree_kernel(tc, x, w1, w2, w3, wo, dy, og, base, out):
 
         def interleave(copy, operand, c0, c1):
             copy(
-                out=operand["grouped"][:, c0:c1, :].rearrange("p (c i) j -> p c j i", i=4),
-                in_=operand["raw"][:, :, c0:c1].rearrange("p j (c i) -> p c j i", i=4),
+                out=operand["grouped"][:, c0:c1, :].rearrange("p (c i) j -> p c j i", i=2),
+                in_=operand["raw"][:, :, c0:c1].rearrange("p j (c i) -> p c j i", i=2),
             )
 
         def quantize(operand, c0, c1):

from contextlib import ExitStack

import concourse.mybir as mybir

G, D, M, N = 2, 256, 128, 512
FLOPS = 4 * 2 * G * D * M * N

F32 = mybir.dt.float32
BF16 = mybir.dt.bfloat16
U32 = mybir.dt.uint32
U8 = mybir.dt.uint8
FP8X4 = mybir.dt.float8_e4m3fn_x4
ACT = mybir.ActivationFunctionType
ALU = mybir.AluOpType

P = 128
PACK = 4
ROWS = D // PACK
HALVES = 2
HALF = N // HALVES
PASS_N = 128
X_SPLIT = 176


def tile_rows_gpsoftmaxthree_kernel(tc, x, w1, w2, w3, wo, dy, og, base, out):
    nc = tc.nc
    with ExitStack() as ctx:
        sb = ctx.enter_context(tc.tile_pool(name="sb", bufs=1))
        ps = ctx.enter_context(tc.psum_pool(name="ps", bufs=1))
        ctx.enter_context(tc.manual_schedule())

        def load(name, src):
            width = src.shape[2]
            raw = sb.tile([P, PACK, width], F32, name=name + "_raw", align_bytes=64)
            nc.sync.dma_start(out=raw[:], in_=src.rearrange("g (p j) w -> (g p) j w", j=PACK))
            grouped = sb.tile([P, width, PACK], BF16, name=name + "_bf", align_bytes=64)
            codes = sb.tile([P, width], U32, name=name + "_codes", align_bytes=64)
            scales = sb.tile([P, width], U8, name=name + "_scales", align_bytes=64)
            return {"raw": raw, "grouped": grouped, "codes": codes, "scales": scales}

        def interleave(copy, operand, c0, c1):
            copy(
                out=operand["grouped"][:, c0:c1, :].rearrange("p (c i) j -> p c j i", i=2),
                in_=operand["raw"][:, :, c0:c1].rearrange("p j (c i) -> p c j i", i=2),
            )

        def quantize(operand, c0, c1):
            nc.vector.quantize_mx(
                out=operand["codes"][:, c0:c1].bitcast(FP8X4),
                scales=operand["scales"][:, c0:c1],
                in_=operand["grouped"][:, c0:c1, :].rearrange("p w j -> p (w j)"),
            )

        def banks(name):
            tiles = []
            for g in range(G):
                t = ps.tile([M, N], F32, name=name + str(g))
                tiles.append(t)
            return tiles

        def product(sums, first, weights, moving, groups):
            width = moving["codes"].shape[1]
            for g in groups:
                rows = slice(g * ROWS, (g + 1) * ROWS)
                for c in range(0, width, PASS_N):
                    nc.tensor.matmul_mx(
                        out=sums[g][:, first + c : first + c + PASS_N],
                        lhsT=weights["codes"][rows, :].bitcast(FP8X4),
                        lhsT_scale=weights["scales"][rows, :],
                        rhs=moving["codes"][rows, c : c + PASS_N].bitcast(FP8X4),
                        rhs_scale=moving["scales"][rows, c : c + PASS_N],
                        start=True,
                        stop=True,
                    )

        def values(name):
            tiles = []
            for h in range(HALVES):
                t = sb.tile([M, G, HALF], F32, name=name + str(h))
                tiles.append(t)
            return tiles

        def fused(dst, a, scalar, op0, b, op1):
            nc.vector.scalar_tensor_tensor(out=dst, in0=a, scalar=scalar, in1=b, op0=op0, op1=op1)

        def binary(dst, a, op, b):
            nc.vector.tensor_tensor(out=dst, in0=a, in1=b, op=op)

        half = [slice(h * HALF, (h + 1) * HALF) for h in range(HALVES)]
        groups = range(G)
        both = slice(0, G)
        xa = load("xa", x[:, :, half[0]])
        w1o = load("w1", w1)
        w2o = load("w2", w2)
        w3o = load("w3", w3)
        xb = load("xb", x[:, :, half[1]])
        woo = load("wo", wo)
        dyo = load("dy", dy)
        base_sb = sb.tile([M, G, N], F32, name="base_sb")
        nc.sync.dma_start(out=base_sb[:], in_=base.rearrange("g m n -> m g n"))
        gain = sb.tile([M, G, 1], F32, name="gain")
        with nc.allow_non_contiguous_dma(reason="one gain per partition and group"):
            nc.sync.dma_start(out=gain[:], in_=og.rearrange("g m o -> m g o"))

        z1, c0 = banks("z1_"), banks("c0_")
        z23 = [banks("z23a_"), banks("z23b_")]
        e23 = []
        for h in range(HALVES):
            pair = sb.tile([M, 2, G, HALF], F32, name="e23_" + str(h))
            e23.append(pair)
        csq = sb.tile([M, G, N], F32, name="csq")
        e1, th, th2 = values("e1"), values("th"), values("th2")
        e12, se, lse, logp, nsl = values("e12"), values("se"), values("lse"), values("logp"), values("nsl")
        prob, sq, tp, a = values("prob"), values("sq"), values("tp"), values("a")
        t1, t2, b, ac, abc, res = values("t1"), values("t2"), values("b"), values("ac"), values("abc"), values("res")

        def exp_z23(h):
            for g in groups:
                nc.scalar.activation(
                    out=e23[h][:, :, g, :], in_=z23[h][g][:].rearrange("m (k n) -> m k n", k=2), func=ACT.Exp
                )

        def step_e12(h):
            binary(e12[h][:], e1[h][:], ALU.add, e23[h][:, 0])

        def step_se(h):
            binary(se[h][:], e12[h][:], ALU.add, e23[h][:, 1])

        def step_logp(h):
            for g in groups:
                binary(logp[h][:, g], z1[g][:, half[h]], ALU.subtract, lse[h][:, g])

        def step_nsl(h, g):
            fused(nsl[h][:, g], th2[h][:, g], 1.0, ALU.subtract, lse[h][:, g], ALU.mult)

        def step_tp(h, g):
            binary(tp[h][:, g], th[h][:, g], ALU.mult, prob[h][:, g])

        def step_a(h, g):
            binary(a[h][:, g], tp[h][:, g], ALU.subtract, nsl[h][:, g])

        def step_t1(h, g):
            fused(t1[h][:, g], a[h][:, g], 2.0, ALU.mult, sq[h][:, g], ALU.add)

        def step_t2(h, g):
            fused(t2[h][:, g], t1[h][:, g], 0.25, ALU.subtract, th[h][:, g], ALU.mult)

        def step_b(h, g):
            fused(b[h][:, g], prob[h][:, g], 2.0, ALU.mult, t2[h][:, g], ALU.subtract)

        def step_ac(h):
            for g in groups:
                fused(ac[h][:, g], a[h][:, g], gain[:, g, :], ALU.mult, csq[:, g, half[h]], ALU.mult)

        def step_abc(h, g):
            fused(abc[h][:, g], ac[h][:, g], 2.0, ALU.mult, b[h][:, g], ALU.mult)

        def step_out(h):
            for g, queue in zip(groups, (nc.sync, nc.scalar)):
                binary(res[h][:, g], abc[h][:, g], ALU.add, base_sb[:, g, half[h]])
                queue.dma_start(out=out[g, :, half[h]], in_=res[h][:, g])

        interleave(nc.vector.tensor_copy, xa, 0, X_SPLIT)
        interleave(nc.scalar.copy, xa, X_SPLIT, HALF)
        interleave(nc.vector.tensor_copy, w1o, 0, M)
        quantize(xa, 0, HALF)
        quantize(w1o, 0, M)
        product(z1, 0, w1o, xa, groups)
        for g in groups:
            nc.scalar.activation(out=e1[0][:, g], in_=z1[g][:, half[0]], func=ACT.Exp)
            nc.scalar.activation(out=th[0][:, g], in_=z1[g][:, half[0]], func=ACT.Tanh)
        interleave(nc.vector.tensor_copy, w2o, 0, M)
        interleave(nc.vector.tensor_copy, w3o, 0, M)
        quantize(w2o, 0, M)
        quantize(w3o, 0, M)
        for g in groups:
            product(z23[0], 0, w2o, xa, [g])
            product(z23[0], HALF, w3o, xa, [g])
        exp_z23(0)
        for c in range(0, HALF, PASS_N):
            interleave(nc.vector.tensor_copy, xb, c, c + PASS_N)
        for c in range(0, HALF, PASS_N):
            quantize(xb, c, c + PASS_N)
        product(z1, HALF, w1o, xb, groups)
        for g in groups:
            product(z23[1], 0, w2o, xb, [g])
            product(z23[1], HALF, w3o, xb, [g])
        for g in groups:
            nc.scalar.activation(out=e1[1][:, g], in_=z1[g][:, half[1]], func=ACT.Exp)
        exp_z23(1)

        binary(th2[0][:], th[0][:], ALU.mult, th[0][:])
        step_e12(0)
        interleave(nc.vector.tensor_copy, woo, 0, M)
        step_se(0)
        step_e12(1)
        quantize(woo, 0, M)
        step_se(1)
        interleave(nc.vector.tensor_copy, dyo, 0, N)
        for h in range(HALVES):
            nc.scalar.activation(out=lse[h][:], in_=se[h][:], func=ACT.Ln)
        step_logp(0)
        quantize(dyo, 0, N)
        product(c0, 0, woo, dyo, groups)
        step_nsl(0, both)
        step_logp(1)

        for g in groups:
            nc.scalar.activation(out=prob[0][:, g], in_=logp[0][:, g], func=ACT.Exp)
        nc.scalar.activation(out=sq[0][:], in_=prob[0][:], func=ACT.Square, bias=-0.5)
        for g in groups:
            nc.scalar.activation(out=th[1][:, g], in_=z1[g][:, half[1]], func=ACT.Tanh)
        nc.scalar.activation(out=prob[1][:], in_=logp[1][:], func=ACT.Exp)
        nc.scalar.activation(out=th2[1][:], in_=th[1][:], func=ACT.Square)
        nc.scalar.activation(out=sq[1][:], in_=prob[1][:], func=ACT.Square, bias=-0.5)
        for g in groups:
            nc.scalar.activation(out=csq[:, g, :], in_=c0[g][:], func=ACT.Square)

        for step in (step_tp, step_a, step_t1):
            for g in groups:
                step(0, g)
        step_tp(1, both)
        step_t2(0, both)
        step_nsl(1, both)
        step_b(0, both)
        step_a(1, both)
        step_ac(0)
        step_t1(1, both)
        step_abc(0, both)
        step_t2(1, both)
        step_out(0)
        step_b(1, both)
        step_ac(1)
        for g in groups:
            step_abc(1, g)
        step_out(1)
